import numpy as np
import ml_dtypes

BF16 = ml_dtypes.bfloat16


def bf(x):
    return np.asarray(x, np.float32).astype(BF16)


def f32(x):
    return np.asarray(x, np.float32)


def f64(x):
    return np.asarray(x).astype(np.float64)


def striped(idx):
    return np.tile(idx.reshape(-1, 16).T, (8, 1))


S, K, M, N, E, Q = 512, 128, 128, 384, 2, 192


def setup_inputs():
    return {"base": bf(np.random.standard_normal((M, S))), "x": bf(np.random.standard_normal((K, N))), "w": bf(np.random.standard_normal((E, K, M)) / np.sqrt(K)), "b": f32(0.5 * np.random.standard_normal((M, 1))), "offs": striped(np.random.permutation(S)[:N])}


def reference(base, x, w, b, offs):
    idx = offs[:16].T.reshape(-1)
    z = f64(base).copy()
    for e in range(E):
        z[:, idx[e * Q : (e + 1) * Q]] += f64(w)[e].T @ f64(x)[:, e * Q : (e + 1) * Q]
    return z + f64(b)

@@ -1,0 +1,50 @@
+import concourse.mybir as mybir
+from concourse.masks import make_identity
+
+BF16, F32, U16 = mybir.dt.bfloat16, mybir.dt.float32, mybir.dt.uint16
+
+P = 128
+TOKENS = 512
+EXPERTS = 2
+PIECE = 192
+PIECE_COLS = PIECE // 16
+
+FLOPS = 2 * P * P * EXPERTS * PIECE
+
+
+def tile_scatter_matmul_kernel(tc, base, x, w, b, offs, out):
+    nc = tc.nc
+    with (
+        tc.tile_pool(name="held", bufs=1) as held,
+        tc.psum_pool(name="psum", bufs=1) as psum,
+    ):
+        offsets = held.tile([P, EXPERTS * PIECE_COLS], U16, name="offsets")
+        nc.sync.dma_start(offsets[:], offs)
+        base_tile = held.tile([P, TOKENS], BF16, name="base_tile")
+        nc.scalar.dma_start(base_tile[:], base)
+        x_tile = held.tile([P, EXPERTS * PIECE], BF16, name="x_tile")
+        nc.sync.dma_start(x_tile[:], x)
+        weights = [held.tile([P, P], BF16, name="weights%d" % e) for e in range(EXPERTS)]
+        nc.scalar.dma_start(weights[0][:], w[0])
+        nc.sync.dma_start(weights[1][:], w[1])
+        bias = held.tile([P, 1], F32, name="bias")
+        nc.scalar.dma_start(bias[:], b)
+
+        identity = held.tile([P, P], BF16, name="identity")
+        make_identity(nc, identity[:])
+
+        window = psum.tile([P, TOKENS], F32, name="window")
+        nc.tensor.matmul(window[:], identity[:], base_tile[:], start=True, stop=False)
+
+        for e in range(EXPERTS):
+            nc.tensor.matmul(
+                window[:].indirect(offsets[:, e * PIECE_COLS : (e + 1) * PIECE_COLS]),
+                weights[e][:],
+                x_tile[:, e * PIECE : (e + 1) * PIECE],
+                start=False,
+                stop=(e == EXPERTS - 1),
+            )
+
+        result = held.tile([P, TOKENS], F32, name="result")
+        nc.vector.tensor_scalar_add(result[:], window[:], bias[:, 0:1])
+        nc.sync.dma_start(out, result[:])

@@ -8,6 +8,7 @@ TOKENS = 512
 EXPERTS = 2
 PIECE = 192
 PIECE_COLS = PIECE // 16
+WARM_UPS = 12
 
 FLOPS = 2 * P * P * EXPERTS * PIECE
 
@@ -32,6 +33,12 @@ def tile_scatter_matmul_kernel(tc, base, x, w, b, offs, out):
 
         identity = held.tile([P, P], BF16, name="identity")
         make_identity(nc, identity[:])
+
+        zeros = held.tile([P, P], BF16, name="zeros")
+        nc.vector.memset(zeros[:], 0.0)
+        unread = psum.tile([P, P], F32, name="unread")
+        for i in range(WARM_UPS):
+            nc.tensor.matmul(unread[:], zeros[:], zeros[:], start=True, stop=True)
 
         window = psum.tile([P, TOKENS], F32, name="window")
         nc.tensor.matmul(window[:], identity[:], base_tile[:], start=True, stop=False)

@@ -5,6 +5,7 @@ BF16, F32, U16 = mybir.dt.bfloat16, mybir.dt.float32, mybir.dt.uint16
 
 P = 128
 TOKENS = 512
+HALF = TOKENS // 2
 EXPERTS = 2
 PIECE = 192
 PIECE_COLS = PIECE // 16
@@ -53,5 +54,7 @@ def tile_scatter_matmul_kernel(tc, base, x, w, b, offs, out):
             )
 
         result = held.tile([P, TOKENS], F32, name="result")
-        nc.vector.tensor_scalar_add(result[:], window[:], bias[:, 0:1])
-        nc.sync.dma_start(out, result[:])
+        for half, queue in enumerate((nc.sync, nc.scalar)):
+            columns = slice(half * HALF, (half + 1) * HALF)
+            nc.vector.tensor_scalar_add(result[:, columns], window[:, columns], bias[:, 0:1])
+            queue.dma_start(out[:, columns], result[:, columns])

@@ -20,12 +20,12 @@ def tile_scatter_matmul_kernel(tc, base, x, w, b, offs, out):
         tc.tile_pool(name="held", bufs=1) as held,
         tc.psum_pool(name="psum", bufs=1) as psum,
     ):
+        base_tile = held.tile([P, TOKENS], BF16, name="base_tile")
+        nc.sync.dma_start(base_tile[:], base)
+        x_tile = held.tile([P, EXPERTS * PIECE], BF16, name="x_tile")
+        nc.scalar.dma_start(x_tile[:], x)
         offsets = held.tile([P, EXPERTS * PIECE_COLS], U16, name="offsets")
         nc.sync.dma_start(offsets[:], offs)
-        base_tile = held.tile([P, TOKENS], BF16, name="base_tile")
-        nc.scalar.dma_start(base_tile[:], base)
-        x_tile = held.tile([P, EXPERTS * PIECE], BF16, name="x_tile")
-        nc.sync.dma_start(x_tile[:], x)
         weights = [held.tile([P, P], BF16, name="weights%d" % e) for e in range(EXPERTS)]
         nc.scalar.dma_start(weights[0][:], w[0])
         nc.sync.dma_start(weights[1][:], w[1])

@@ -9,7 +9,8 @@ HALF = TOKENS // 2
 EXPERTS = 2
 PIECE = 192
 PIECE_COLS = PIECE // 16
-WARM_UPS = 12
+GROUP = 32
+WARM_UPS = 3
 
 FLOPS = 2 * P * P * EXPERTS * PIECE
 
@@ -35,11 +36,18 @@ def tile_scatter_matmul_kernel(tc, base, x, w, b, offs, out):
         identity = held.tile([P, P], BF16, name="identity")
         make_identity(nc, identity[:])
 
-        zeros = held.tile([P, P], BF16, name="zeros")
+        zeros = held.tile([P, 1], BF16, name="zeros")
         nc.vector.memset(zeros[:], 0.0)
-        unread = psum.tile([P, P], F32, name="unread")
+        unread = psum.tile([P, TOKENS], F32, name="unread")
         for i in range(WARM_UPS):
-            nc.tensor.matmul(unread[:], zeros[:], zeros[:], start=True, stop=True)
+            for first in range(0, P, GROUP):
+                nc.tensor.matmul(
+                    unread[first : first + GROUP, :],
+                    zeros[:, 0:1].to_broadcast([P, GROUP]),
+                    zeros[:, 0:1].to_broadcast([P, TOKENS]),
+                    start=True,
+                    stop=True,
+                )
 
         window = psum.tile([P, TOKENS], F32, name="window")
         nc.tensor.matmul(window[:], identity[:], base_tile[:], start=True, stop=False)

@@ -10,7 +10,7 @@ EXPERTS = 2
 PIECE = 192
 PIECE_COLS = PIECE // 16
 GROUP = 32
-WARM_UPS = 3
+WARM_UPS = 2
 
 FLOPS = 2 * P * P * EXPERTS * PIECE
 

import concourse.mybir as mybir
from concourse.masks import make_identity

BF16, F32, U16 = mybir.dt.bfloat16, mybir.dt.float32, mybir.dt.uint16

P = 128
TOKENS = 512
HALF = TOKENS // 2
EXPERTS = 2
PIECE = 192
PIECE_COLS = PIECE // 16
GROUP = 32
WARM_UPS = 2

FLOPS = 2 * P * P * EXPERTS * PIECE


def tile_scatter_matmul_kernel(tc, base, x, w, b, offs, out):
    nc = tc.nc
    with (
        tc.tile_pool(name="held", bufs=1) as held,
        tc.psum_pool(name="psum", bufs=1) as psum,
    ):
        base_tile = held.tile([P, TOKENS], BF16, name="base_tile")
        nc.sync.dma_start(base_tile[:], base)
        x_tile = held.tile([P, EXPERTS * PIECE], BF16, name="x_tile")
        nc.scalar.dma_start(x_tile[:], x)
        offsets = held.tile([P, EXPERTS * PIECE_COLS], U16, name="offsets")
        nc.sync.dma_start(offsets[:], offs)
        weights = [held.tile([P, P], BF16, name="weights%d" % e) for e in range(EXPERTS)]
        nc.scalar.dma_start(weights[0][:], w[0])
        nc.sync.dma_start(weights[1][:], w[1])
        bias = held.tile([P, 1], F32, name="bias")
        nc.scalar.dma_start(bias[:], b)

        identity = held.tile([P, P], BF16, name="identity")
        make_identity(nc, identity[:])

        zeros = held.tile([P, 1], BF16, name="zeros")
        nc.vector.memset(zeros[:], 0.0)
        unread = psum.tile([P, TOKENS], F32, name="unread")
        for i in range(WARM_UPS):
            for first in range(0, P, GROUP):
                nc.tensor.matmul(
                    unread[first : first + GROUP, :],
                    zeros[:, 0:1].to_broadcast([P, GROUP]),
                    zeros[:, 0:1].to_broadcast([P, TOKENS]),
                    start=True,
                    stop=True,
                )

        window = psum.tile([P, TOKENS], F32, name="window")
        nc.tensor.matmul(window[:], identity[:], base_tile[:], start=True, stop=False)

        for e in range(EXPERTS):
            nc.tensor.matmul(
                window[:].indirect(offsets[:, e * PIECE_COLS : (e + 1) * PIECE_COLS]),
                weights[e][:],
                x_tile[:, e * PIECE : (e + 1) * PIECE],
                start=False,
                stop=(e == EXPERTS - 1),
            )

        result = held.tile([P, TOKENS], F32, name="result")
        for half, queue in enumerate((nc.sync, nc.scalar)):
            columns = slice(half * HALF, (half + 1) * HALF)
            nc.vector.tensor_scalar_add(result[:, columns], window[:, columns], bias[:, 0:1])
            queue.dma_start(out[:, columns], result[:, columns])
